import numpy as np
import ml_dtypes


def mxq(x, axis, fmt="e4m3"):
    dtype, down = {"e4m3": (ml_dtypes.float8_e4m3fn, 7), "e5m2": (ml_dtypes.float8_e5m2, 14)}[fmt]
    v = np.moveaxis(np.asarray(x, np.float32).astype(ml_dtypes.bfloat16).astype(np.float64), axis, -1)
    blocks = v.reshape(v.shape[:-1] + (-1, 32))
    amax = np.abs(blocks).max(-1, keepdims=True)
    byte = np.maximum(np.where(amax > 0, np.frexp(amax)[1] - 1 + 127, 0) - down, 1)
    scale = np.exp2(byte - 127.0)
    codes = (blocks / scale).astype(np.float32).astype(dtype).astype(np.float64)
    return np.moveaxis((codes * scale).reshape(v.shape), -1, axis)


WIDE = False


def mx_kscale(k):
    if not WIDE:
        return np.ones(k)
    levels = np.array([10, -10, 5, -5, 0])
    if k % 512:
        return np.exp2(np.random.permutation(np.resize(levels, k // 32))).repeat(32)
    a = np.empty((k // 512, 16))
    for p in range(k // 512):
        a[p, :8] = np.random.permutation(np.resize(levels, 8))
        for g in range(8):
            far = levels[np.abs(levels - a[p, g]) >= 10]
            a[p, g + 8] = far[np.random.randint(len(far))]
    return np.exp2(a.ravel()).repeat(32)


def f64(x):
    return np.asarray(x).astype(np.float64)


def striped(idx):
    return np.tile(np.asarray(idx).reshape(-1, 16).T, (8, 1)).astype(np.uint16)


def unstriped(offs):
    return offs[:16].T.reshape(-1).astype(np.int64)


def striped8(idx):
    return np.asarray(idx).reshape(8, -1, 16).transpose(0, 2, 1).reshape(128, -1).astype(np.uint16)


def unstriped8(offs):
    return offs.reshape(8, 16, -1).transpose(0, 2, 1).reshape(8, -1).astype(np.int64)


def pick8(x, idx, run):
    r = np.arange(len(x))
    return x[r[:, None], idx[r % (8 * run) // run]]


E2M1 = np.array([0.0, 0.5, 1.0, 1.5, 2.0, 3.0, 4.0, 6.0, -0.0, -0.5, -1.0, -1.5, -2.0, -3.0, -4.0, -6.0])


def pack_weight(w, fmt):
    k, n = w.shape
    w = f64(np.asarray(w, np.float32).astype(ml_dtypes.bfloat16)).reshape(k // 32, 32, n)
    amax = np.abs(w).max(1)
    if fmt == "e4m3":
        byte = np.frexp(amax)[1] - 1 + 127 - 7
    else:
        mant, ex = np.frexp(amax / 6.0)
        byte = np.where(mant > 0.5, ex, ex - 1) + 127
    byte = np.clip(np.where(amax > 0, byte, 1), 1, 254)
    scaled = (w * np.exp2(127.0 - byte)[:, None, :]).reshape(k, n).astype(np.float32)
    by_word = np.ascontiguousarray(scaled.reshape(k // 512, 128, 4, n).transpose(0, 1, 3, 2))
    if fmt == "e4m3":
        words = by_word.astype(ml_dtypes.float8_e4m3fn).view(np.uint8)
    else:
        c = by_word.astype(ml_dtypes.float4_e2m1fn).view(np.uint8) & 0xF
        words = (c[..., 0::2] | (c[..., 1::2] << 4)).reshape(k // 512, 128, 2 * n)
    return np.ascontiguousarray(words), np.ascontiguousarray(byte.astype(np.uint8).reshape(k // 512, 16, n))


def unpack_weight(words, scales, fmt):
    g, _, n = scales.shape
    words = np.ascontiguousarray(words).reshape(g, 128, n, -1)
    if fmt == "e4m3":
        vals = words.view(ml_dtypes.float8_e4m3fn).astype(np.float64)
    else:
        nib = np.empty((g, 128, n, 4), np.uint8)
        nib[..., 0::2] = words & 0xF
        nib[..., 1::2] = words >> 4
        vals = E2M1[nib]
    vals = vals * np.repeat(np.exp2(scales.astype(np.float64) - 127.0), 8, axis=1)[..., None]
    return vals.transpose(0, 1, 3, 2).reshape(g * 512, n)


K, J, R, T, F, O, N, U = 512, 512, 512, 2048, 2048, 256, 256, 128


def setup_inputs():
    n = np.random.standard_normal
    idx = np.stack([np.random.permutation(T)[:J] for _ in range(8)])
    idx2 = np.stack([np.random.permutation(T)[:J] for _ in range(8)])
    idx3 = np.stack([np.random.permutation(F)[:R] for _ in range(8)])
    idx4 = np.random.permutation(J)[:O]
    idx5 = np.stack([np.random.permutation(J)[:O] for _ in range(8)])
    idx6 = np.stack([np.random.permutation(O)[:U] for _ in range(8)])
    idx7 = np.stack([np.random.permutation(O)[:U] for _ in range(8)])
    fk = mx_kscale(K)
    fr = mx_kscale(R)
    wbp = pack_weight(n((R, N)) * 1 / np.sqrt(R) / fr[:, None], "e2m1")
    wop = pack_weight(n((R, N)) * 1 / np.sqrt(R) / fr[:, None], "e4m3")
    return {
        "ta": (np.random.randint(-7, 8, (K, T)).astype(np.float64)).astype(np.float32),
        "ga": ((np.random.randint(10, 25, (K, 1)) / 64.0) * fk[:, None]).astype(np.float32),
        "gb": ((np.random.randint(4, 13, (K, 1)) / 64.0) * fk[:, None]).astype(np.float32),
        "ua": (np.random.randint(-7, 8, (K, F)).astype(np.float64)).astype(np.float32),
        "ha": ((np.random.randint(8, 25, (K, 1)) / 1024.0) / fk[:, None]).astype(np.float32),
        "sa": (np.random.uniform(0.5, 1.6, (R, 1)) * fr[:, None]).astype(np.float32),
        "sb": (np.random.uniform(0.5, 1.6, (R, 1)) * fr[:, None]).astype(np.float32),
        "wb_words": wbp[0],
        "wb_scales": wbp[1],
        "wo_words": wop[0],
        "wo_scales": wop[1],
        "so": (np.random.uniform(0.5, 1.6, (N, 1))).astype(np.float32),
        "sp": (np.random.uniform(0.5, 1.6, (N, 1))).astype(np.float32),
        "offs": striped8(idx),
        "offs2": striped8(idx2),
        "offs3": striped8(idx3),
        "offs4": striped(idx4),
        "offs5": striped8(idx5),
        "offs6": striped8(idx6),
        "offs7": striped8(idx7),
    }


def reference(ta, ga, gb, ua, ha, sa, sb, wb_words, wb_scales, wo_words, wo_scales, so, sp, offs, offs2, offs3, offs4, offs5, offs6, offs7):
    idx = unstriped8(offs)
    idx2 = unstriped8(offs2)
    idx3 = unstriped8(offs3)
    idx4 = unstriped(offs4)
    idx5 = unstriped8(offs5)
    idx6 = unstriped8(offs6)
    idx7 = unstriped8(offs7)
    wbu = unpack_weight(wb_words, wb_scales, "e2m1")
    wou = unpack_weight(wo_words, wo_scales, "e4m3")
    xc = pick8(f64(ta), idx, 64) * f64(ga) + pick8(f64(ta), idx2, 64) * f64(gb)
    wc = pick8(f64(ua), idx3, 64) * f64(ha)
    wcq = mxq(wc, 0, "e4m3")
    xcq = mxq(xc, 0, "e4m3")
    a = wcq.T @ xcq
    hid = np.maximum(a[:, idx4] * f64(sa), pick8(a, idx5, 64) * f64(sb))
    hidq = mxq(hid, 0, "e4m3")
    p = wbu.T @ hidq
    q = wou.T @ hidq
    y = pick8(p, idx6, 16) * f64(so) - pick8(q, idx7, 16) * f64(sp)
    return y

@@ -1,0 +1,217 @@
+from contextlib import ExitStack
+
+import concourse.mybir as mybir
+
+K, J, R, T, F, O, N, U = 512, 512, 512, 2048, 2048, 256, 256, 128
+FLOPS = 2 * K * R * J + 2 * 2 * R * N * O
+
+F32 = mybir.dt.float32
+BF16 = mybir.dt.bfloat16
+I32 = mybir.dt.int32
+U32 = mybir.dt.uint32
+U16 = mybir.dt.uint16
+U8 = mybir.dt.uint8
+FP8X4 = mybir.dt.float8_e4m3fn_x4
+FP4X4 = mybir.dt.float4_e2m1fn_x4
+COPY = mybir.ActivationFunctionType.Copy
+ALU = mybir.AluOpType
+
+P = 128
+PACK = 4
+HALF = O // 2
+LIST = 16
+
+
+def tile_picked_refined_codes_one_mixedpair_outcomes_outmeet_kernel(
+    tc, ta, ga, gb, ua, ha, sa, sb, wb_words, wb_scales, wo_words, wo_scales, so, sp,
+    offs, offs2, offs3, offs4, offs5, offs6, offs7, out,
+):
+    nc = tc.nc
+    with ExitStack() as ctx:
+        keep = ctx.enter_context(tc.tile_pool(name="keep", bufs=1))
+        psum = ctx.enter_context(tc.psum_pool(name="psum", bufs=1))
+
+        def sb_tile(name, shape, dtype):
+            return keep.tile(shape, dtype, name=name, align_bytes=64)
+
+        def load_list(name, src):
+            tile = sb_tile(name, list(src.shape), U16)
+            nc.sync.dma_start(tile[:], src)
+            return tile
+
+        def load_by_slot(name, src, queue):
+            tile = sb_tile(name, [P, PACK], F32)
+            queue.dma_start(tile[:], src.rearrange("(p t) o -> p (t o)", t=PACK))
+            return tile
+
+        def load_rows(name, src, t):
+            tile = sb_tile(name, [P, src.shape[1]], F32)
+            nc.sync.dma_start(tile[:], src.rearrange("(p t) c -> p t c", t=PACK)[:, t, :])
+            return tile
+
+        def load_by_tile(name, src):
+            tile = sb_tile(name, [P, N // P, 1], F32)
+            with nc.allow_non_contiguous_dma(reason="one value a partition for each tile of 128 output features"):
+                nc.sync.dma_start(tile[:], src.rearrange("(i p) o -> p i o", p=P))
+            return tile
+
+        def load_scale_rows(name, src):
+            tile = sb_tile(name, [4, 4, N // 4], I32)
+            nc.sync.dma_start(tile[:], src[0].bitcast(I32).rearrange("(q r) c -> r q c", r=4))
+            return tile
+
+        def spread_scale_rows(name, rows):
+            plane = sb_tile(name, [P, N // 4], I32)
+            nc.vector.memset(plane[:], 0)
+            for q in range(4):
+                nc.vector.tensor_copy(plane[32 * q : 32 * q + 4, :], rows[:, q, :])
+            return plane[:].bitcast(U8)
+
+        def gather(dst, window, offsets, scale):
+            nc.scalar.activation(out=dst, in_=window[:].indirect(offsets), func=COPY, scale=scale)
+
+        def quantise(name, src, cols):
+            codes = sb_tile(name + "_codes", [P, cols], U32)
+            scales = sb_tile(name + "_scales", [P, cols], U8)
+            nc.vector.quantize_mx(
+                out=codes[:].bitcast(FP8X4), scales=scales[:], in_=src[:].rearrange("p c t -> p (c t)")
+            )
+            return codes, scales
+
+        ga_t = load_by_slot("ga_t", ga, nc.scalar)
+        gb_t = load_by_slot("gb_t", gb, nc.scalar)
+        ta_t = [load_rows("ta0", ta, 0)]
+        l1 = load_list("l1", offs)
+        l2 = load_list("l2", offs2)
+        ta_t.extend(load_rows("ta%d" % t, ta, t) for t in range(1, PACK))
+        l3 = load_list("l3", offs3)
+        ha_t = load_by_slot("ha_t", ha, nc.sync)
+        wb_rows = load_scale_rows("wb_rows", wb_scales)
+        wo_rows = load_scale_rows("wo_rows", wo_scales)
+        ua_t = [load_rows("ua%d" % t, ua, t) for t in range(PACK)]
+        l4 = load_list("l4", offs4)
+        l5 = load_list("l5", offs5)
+        sa_t = load_by_slot("sa_t", sa, nc.sync)
+        sb_t = load_by_slot("sb_t", sb, nc.sync)
+        wb_w = sb_tile("wb_w", [P, 2 * N], U8)
+        nc.sync.dma_start(wb_w[:].bitcast(I32), wb_words[0].bitcast(I32))
+        wo_w = sb_tile("wo_w", [P, PACK * N], U8)
+        nc.sync.dma_start(wo_w[:].bitcast(I32), wo_words[0].rearrange("p n t -> p (n t)").bitcast(I32))
+        l6 = load_list("l6", offs6)
+        l7 = load_list("l7", offs7)
+        so_t = load_by_tile("so_t", so)
+        sp_t = load_by_tile("sp_t", sp)
+
+        x_planes = sb_tile("x_planes", [P, PACK, J], BF16)
+        for t in range(PACK):
+            coarse = sb_tile("coarse%d" % t, [P, J], F32)
+            fine = sb_tile("fine%d" % t, [P, J], F32)
+            gather(coarse[:], ta_t[t], l1[:], ga_t[:, t : t + 1])
+            gather(fine[:], ta_t[t], l2[:], gb_t[:, t : t + 1])
+            nc.vector.tensor_tensor(x_planes[:, t, :], coarse[:], fine[:], ALU.add)
+        x_words = sb_tile("x_words", [P, J, PACK], BF16)
+        nc.vector.tensor_copy(x_words[:], x_planes[:].rearrange("p t j -> p j t"))
+        x_codes, x_scales = quantise("x", x_words, J)
+        wb_s = spread_scale_rows("wb_s", wb_rows)
+        wo_s = spread_scale_rows("wo_s", wo_rows)
+
+        w_words = [sb_tile("w_words%d" % s, [P, P, PACK], BF16) for s in range(PACK)]
+        w_plane = None
+        for t in range(PACK):
+            w_plane = sb_tile("w_plane%d" % t, [P, P, PACK], BF16)
+            gather(w_plane[:].rearrange("p m s -> p (m s)"), ua_t[t], l3[:], ha_t[:, t : t + 1])
+            if t < PACK - 1:
+                for s in range(PACK):
+                    nc.vector.tensor_copy(w_words[s][:, :, t], w_plane[:, :, s])
+
+        a_rows = [sb_tile("a_rows%d" % s, [P, J], F32) for s in range(PACK)]
+        w_q = []
+        nc.vector.tensor_copy(w_words[0][:, :, PACK - 1], w_plane[:, :, 0])
+        for s in range(PACK):
+            if s + 1 < PACK:
+                nc.vector.tensor_copy(w_words[s + 1][:, :, PACK - 1], w_plane[:, :, s + 1])
+            w_q.append(quantise("w%d" % s, w_words[s], P))
+
+        def first_product(s, bank, cols):
+            acc = psum.tile([P, cols.stop - cols.start], F32, name="a_ps%d_%d" % (s, cols.start), tag="bank%d" % bank)
+            nc.tensor.matmul_mx(
+                out=acc[:],
+                lhsT=w_q[s][0][:].bitcast(FP8X4), lhsT_scale=w_q[s][1][:],
+                rhs=x_codes[:, cols].bitcast(FP8X4), rhs_scale=x_scales[:, cols],
+                start=True, stop=True,
+            )
+            return acc
+
+        lo, hi = slice(0, J // 2), slice(J // 2, J)
+        acc_lo = first_product(0, 0, lo)
+        acc_hi = first_product(0, 1, hi)
+        nc.scalar.copy(a_rows[0][:, lo], acc_lo[:])
+        nc.vector.tensor_copy(a_rows[0][:, hi], acc_hi[:])
+        for s in range(1, PACK):
+            acc = first_product(s, s + 1, slice(0, J))
+            nc.vector.tensor_copy(a_rows[s][:], acc[:])
+
+        one01 = sb_tile("one01", [P, 2, O], F32)
+        own01 = sb_tile("own01", [P, 2, O], F32)
+        for s in range(2):
+            gather(one01[:, s, :], a_rows[s], l4[:], sa_t[:, s : s + 1])
+            gather(own01[:, s, :], a_rows[s], l5[:], sb_t[:, s : s + 1])
+
+        p_rows = [sb_tile("p_rows%d" % i, [P, O], F32) for i in range(N // P)]
+        q_rows = [sb_tile("q_rows%d" % i, [P, O], F32) for i in range(N // P)]
+        second = []
+        for i in range(N // P):
+            cols = slice(i * P, (i + 1) * P)
+            second.append((wb_w[:, 2 * i * P : 2 * (i + 1) * P].bitcast(FP4X4), wb_s[:, cols], p_rows[i]))
+            second.append((wo_w[:, PACK * i * P : PACK * (i + 1) * P].bitcast(FP8X4), wo_s[:, cols], q_rows[i]))
+
+        hid_q = []
+        for h in range(2):
+            one23 = sb_tile("one23_%d" % h, [P, 2, HALF], F32)
+            own23 = sb_tile("own23_%d" % h, [P, 2, HALF], F32)
+            part = slice(h * HALF // LIST, (h + 1) * HALF // LIST)
+            for s in range(2, PACK):
+                gather(one23[:, s - 2, :], a_rows[s], l4[:, part], sa_t[:, s : s + 1])
+                gather(own23[:, s - 2, :], a_rows[s], l5[:, part], sb_t[:, s : s + 1])
+            hid_words = keep.tile([P, HALF, PACK], BF16, name="hid_words%d" % h, tag="hid_words", align_bytes=64)
+            cols = slice(h * HALF, (h + 1) * HALF)
+            nc.vector.tensor_tensor(
+                hid_words[:, :, 0:2],
+                one01[:, :, cols].rearrange("p s o -> p o s"),
+                own01[:, :, cols].rearrange("p s o -> p o s"),
+                ALU.max,
+            )
+            nc.vector.tensor_tensor(
+                hid_words[:, :, 2:4],
+                one23[:].rearrange("p s o -> p o s"),
+                own23[:].rearrange("p s o -> p o s"),
+                ALU.max,
+            )
+            hid_q.append(quantise("hid%d" % h, hid_words, HALF))
+
+        def second_product(acc, m, h):
+            nc.tensor.matmul_mx(
+                out=acc,
+                lhsT=second[m][0], lhsT_scale=second[m][1],
+                rhs=hid_q[h][0][:].bitcast(FP8X4), rhs_scale=hid_q[h][1][:],
+                start=True, stop=True,
+            )
+
+        early = psum.tile([P, len(second), HALF], F32, name="early", tag="bank5")
+        for m in range(len(second)):
+            second_product(early[:, m, :], m, 0)
+        for m in range(len(second)):
+            nc.scalar.copy(second[m][2][:, 0:HALF], early[:, m, :])
+        for m in range(len(second)):
+            late = psum.tile([P, HALF], F32, name="late%d" % m, tag="bank%d" % ((6 + m) % 8))
+            second_product(late[:], m, 1)
+            nc.vector.tensor_copy(second[m][2][:, HALF:O], late[:])
+
+        for i in range(N // P):
+            p_pick = sb_tile("p_pick%d" % i, [P, U], F32)
+            q_pick = sb_tile("q_pick%d" % i, [P, U], F32)
+            res = sb_tile("res%d" % i, [P, U], F32)
+            gather(p_pick[:], p_rows[i], l6[:], so_t[:, i, :])
+            gather(q_pick[:], q_rows[i], l7[:], sp_t[:, i, :])
+            nc.vector.tensor_tensor(res[:], p_pick[:], q_pick[:], ALU.subtract)
+            nc.sync.dma_start(out[i * P : (i + 1) * P, :], res[:])

@@ -57,7 +57,7 @@ def tile_picked_refined_codes_one_mixedpair_outcomes_outmeet_kernel(
 
         def load_scale_rows(name, src):
             tile = sb_tile(name, [4, 4, N // 4], I32)
-            nc.sync.dma_start(tile[:], src[0].bitcast(I32).rearrange("(q r) c -> r q c", r=4))
+            nc.gpsimd.dma_start(tile[:], src[0].bitcast(I32).rearrange("(q r) c -> r q c", r=4))
             return tile
 
         def spread_scale_rows(name, rows):
@@ -80,14 +80,14 @@ def tile_picked_refined_codes_one_mixedpair_outcomes_outmeet_kernel(
 
         ga_t = load_by_slot("ga_t", ga, nc.scalar)
         gb_t = load_by_slot("gb_t", gb, nc.scalar)
+        ha_t = load_by_slot("ha_t", ha, nc.gpsimd)
+        wb_rows = load_scale_rows("wb_rows", wb_scales)
+        wo_rows = load_scale_rows("wo_rows", wo_scales)
         ta_t = [load_rows("ta0", ta, 0)]
         l1 = load_list("l1", offs)
         l2 = load_list("l2", offs2)
         ta_t.extend(load_rows("ta%d" % t, ta, t) for t in range(1, PACK))
         l3 = load_list("l3", offs3)
-        ha_t = load_by_slot("ha_t", ha, nc.sync)
-        wb_rows = load_scale_rows("wb_rows", wb_scales)
-        wo_rows = load_scale_rows("wo_rows", wo_scales)
         ua_t = [load_rows("ua%d" % t, ua, t) for t in range(PACK)]
         l4 = load_list("l4", offs4)
         l5 = load_list("l5", offs5)
@@ -151,12 +151,6 @@ def tile_picked_refined_codes_one_mixedpair_outcomes_outmeet_kernel(
             acc = first_product(s, s + 1, slice(0, J))
             nc.vector.tensor_copy(a_rows[s][:], acc[:])
 
-        one01 = sb_tile("one01", [P, 2, O], F32)
-        own01 = sb_tile("own01", [P, 2, O], F32)
-        for s in range(2):
-            gather(one01[:, s, :], a_rows[s], l4[:], sa_t[:, s : s + 1])
-            gather(own01[:, s, :], a_rows[s], l5[:], sb_t[:, s : s + 1])
-
         p_rows = [sb_tile("p_rows%d" % i, [P, O], F32) for i in range(N // P)]
         q_rows = [sb_tile("q_rows%d" % i, [P, O], F32) for i in range(N // P)]
         second = []
@@ -167,26 +161,20 @@ def tile_picked_refined_codes_one_mixedpair_outcomes_outmeet_kernel(
 
         hid_q = []
         for h in range(2):
-            one23 = sb_tile("one23_%d" % h, [P, 2, HALF], F32)
-            own23 = sb_tile("own23_%d" % h, [P, 2, HALF], F32)
+            hid_words = sb_tile("hid_words%d" % h, [P, HALF, PACK], BF16)
             part = slice(h * HALF // LIST, (h + 1) * HALF // LIST)
-            for s in range(2, PACK):
-                gather(one23[:, s - 2, :], a_rows[s], l4[:, part], sa_t[:, s : s + 1])
-                gather(own23[:, s - 2, :], a_rows[s], l5[:, part], sb_t[:, s : s + 1])
-            hid_words = keep.tile([P, HALF, PACK], BF16, name="hid_words%d" % h, tag="hid_words", align_bytes=64)
-            cols = slice(h * HALF, (h + 1) * HALF)
-            nc.vector.tensor_tensor(
-                hid_words[:, :, 0:2],
-                one01[:, :, cols].rearrange("p s o -> p o s"),
-                own01[:, :, cols].rearrange("p s o -> p o s"),
-                ALU.max,
-            )
-            nc.vector.tensor_tensor(
-                hid_words[:, :, 2:4],
-                one23[:].rearrange("p s o -> p o s"),
-                own23[:].rearrange("p s o -> p o s"),
-                ALU.max,
-            )
+            for s0 in range(0, PACK, 2):
+                shared = keep.tile([P, 2, HALF], F32, name="shared%d_%d" % (h, s0), tag="shared%d" % s0)
+                own = keep.tile([P, 2, HALF], F32, name="own%d_%d" % (h, s0), tag="own%d" % s0)
+                for s in range(s0, s0 + 2):
+                    gather(shared[:, s - s0, :], a_rows[s], l4[:, part], sa_t[:, s : s + 1])
+                    gather(own[:, s - s0, :], a_rows[s], l5[:, part], sb_t[:, s : s + 1])
+                nc.vector.tensor_tensor(
+                    hid_words[:, :, s0 : s0 + 2],
+                    shared[:].rearrange("p s o -> p o s"),
+                    own[:].rearrange("p s o -> p o s"),
+                    ALU.max,
+                )
             hid_q.append(quantise("hid%d" % h, hid_words, HALF))
 
         def second_product(acc, m, h):

from contextlib import ExitStack

import concourse.mybir as mybir

K, J, R, T, F, O, N, U = 512, 512, 512, 2048, 2048, 256, 256, 128
FLOPS = 2 * K * R * J + 2 * 2 * R * N * O

F32 = mybir.dt.float32
BF16 = mybir.dt.bfloat16
I32 = mybir.dt.int32
U32 = mybir.dt.uint32
U16 = mybir.dt.uint16
U8 = mybir.dt.uint8
FP8X4 = mybir.dt.float8_e4m3fn_x4
FP4X4 = mybir.dt.float4_e2m1fn_x4
COPY = mybir.ActivationFunctionType.Copy
ALU = mybir.AluOpType

P = 128
PACK = 4
HALF = O // 2
LIST = 16


def tile_picked_refined_codes_one_mixedpair_outcomes_outmeet_kernel(
    tc, ta, ga, gb, ua, ha, sa, sb, wb_words, wb_scales, wo_words, wo_scales, so, sp,
    offs, offs2, offs3, offs4, offs5, offs6, offs7, out,
):
    nc = tc.nc
    with ExitStack() as ctx:
        keep = ctx.enter_context(tc.tile_pool(name="keep", bufs=1))
        psum = ctx.enter_context(tc.psum_pool(name="psum", bufs=1))

        def sb_tile(name, shape, dtype):
            return keep.tile(shape, dtype, name=name, align_bytes=64)

        def load_list(name, src):
            tile = sb_tile(name, list(src.shape), U16)
            nc.sync.dma_start(tile[:], src)
            return tile

        def load_by_slot(name, src, queue):
            tile = sb_tile(name, [P, PACK], F32)
            queue.dma_start(tile[:], src.rearrange("(p t) o -> p (t o)", t=PACK))
            return tile

        def load_rows(name, src, t):
            tile = sb_tile(name, [P, src.shape[1]], F32)
            nc.sync.dma_start(tile[:], src.rearrange("(p t) c -> p t c", t=PACK)[:, t, :])
            return tile

        def load_by_tile(name, src):
            tile = sb_tile(name, [P, N // P, 1], F32)
            with nc.allow_non_contiguous_dma(reason="one value a partition for each tile of 128 output features"):
                nc.sync.dma_start(tile[:], src.rearrange("(i p) o -> p i o", p=P))
            return tile

        def load_scale_rows(name, src):
            tile = sb_tile(name, [4, 4, N // 4], I32)
            nc.gpsimd.dma_start(tile[:], src[0].bitcast(I32).rearrange("(q r) c -> r q c", r=4))
            return tile

        def spread_scale_rows(name, rows):
            plane = sb_tile(name, [P, N // 4], I32)
            nc.vector.memset(plane[:], 0)
            for q in range(4):
                nc.vector.tensor_copy(plane[32 * q : 32 * q + 4, :], rows[:, q, :])
            return plane[:].bitcast(U8)

        def gather(dst, window, offsets, scale):
            nc.scalar.activation(out=dst, in_=window[:].indirect(offsets), func=COPY, scale=scale)

        def quantise(name, src, cols):
            codes = sb_tile(name + "_codes", [P, cols], U32)
            scales = sb_tile(name + "_scales", [P, cols], U8)
            nc.vector.quantize_mx(
                out=codes[:].bitcast(FP8X4), scales=scales[:], in_=src[:].rearrange("p c t -> p (c t)")
            )
            return codes, scales

        ga_t = load_by_slot("ga_t", ga, nc.scalar)
        gb_t = load_by_slot("gb_t", gb, nc.scalar)
        ha_t = load_by_slot("ha_t", ha, nc.gpsimd)
        wb_rows = load_scale_rows("wb_rows", wb_scales)
        wo_rows = load_scale_rows("wo_rows", wo_scales)
        ta_t = [load_rows("ta0", ta, 0)]
        l1 = load_list("l1", offs)
        l2 = load_list("l2", offs2)
        ta_t.extend(load_rows("ta%d" % t, ta, t) for t in range(1, PACK))
        l3 = load_list("l3", offs3)
        ua_t = [load_rows("ua%d" % t, ua, t) for t in range(PACK)]
        l4 = load_list("l4", offs4)
        l5 = load_list("l5", offs5)
        sa_t = load_by_slot("sa_t", sa, nc.sync)
        sb_t = load_by_slot("sb_t", sb, nc.sync)
        wb_w = sb_tile("wb_w", [P, 2 * N], U8)
        nc.sync.dma_start(wb_w[:].bitcast(I32), wb_words[0].bitcast(I32))
        wo_w = sb_tile("wo_w", [P, PACK * N], U8)
        nc.sync.dma_start(wo_w[:].bitcast(I32), wo_words[0].rearrange("p n t -> p (n t)").bitcast(I32))
        l6 = load_list("l6", offs6)
        l7 = load_list("l7", offs7)
        so_t = load_by_tile("so_t", so)
        sp_t = load_by_tile("sp_t", sp)

        x_planes = sb_tile("x_planes", [P, PACK, J], BF16)
        for t in range(PACK):
            coarse = sb_tile("coarse%d" % t, [P, J], F32)
            fine = sb_tile("fine%d" % t, [P, J], F32)
            gather(coarse[:], ta_t[t], l1[:], ga_t[:, t : t + 1])
            gather(fine[:], ta_t[t], l2[:], gb_t[:, t : t + 1])
            nc.vector.tensor_tensor(x_planes[:, t, :], coarse[:], fine[:], ALU.add)
        x_words = sb_tile("x_words", [P, J, PACK], BF16)
        nc.vector.tensor_copy(x_words[:], x_planes[:].rearrange("p t j -> p j t"))
        x_codes, x_scales = quantise("x", x_words, J)
        wb_s = spread_scale_rows("wb_s", wb_rows)
        wo_s = spread_scale_rows("wo_s", wo_rows)

        w_words = [sb_tile("w_words%d" % s, [P, P, PACK], BF16) for s in range(PACK)]
        w_plane = None
        for t in range(PACK):
            w_plane = sb_tile("w_plane%d" % t, [P, P, PACK], BF16)
            gather(w_plane[:].rearrange("p m s -> p (m s)"), ua_t[t], l3[:], ha_t[:, t : t + 1])
            if t < PACK - 1:
                for s in range(PACK):
                    nc.vector.tensor_copy(w_words[s][:, :, t], w_plane[:, :, s])

        a_rows = [sb_tile("a_rows%d" % s, [P, J], F32) for s in range(PACK)]
        w_q = []
        nc.vector.tensor_copy(w_words[0][:, :, PACK - 1], w_plane[:, :, 0])
        for s in range(PACK):
            if s + 1 < PACK:
                nc.vector.tensor_copy(w_words[s + 1][:, :, PACK - 1], w_plane[:, :, s + 1])
            w_q.append(quantise("w%d" % s, w_words[s], P))

        def first_product(s, bank, cols):
            acc = psum.tile([P, cols.stop - cols.start], F32, name="a_ps%d_%d" % (s, cols.start), tag="bank%d" % bank)
            nc.tensor.matmul_mx(
                out=acc[:],
                lhsT=w_q[s][0][:].bitcast(FP8X4), lhsT_scale=w_q[s][1][:],
                rhs=x_codes[:, cols].bitcast(FP8X4), rhs_scale=x_scales[:, cols],
                start=True, stop=True,
            )
            return acc

        lo, hi = slice(0, J // 2), slice(J // 2, J)
        acc_lo = first_product(0, 0, lo)
        acc_hi = first_product(0, 1, hi)
        nc.scalar.copy(a_rows[0][:, lo], acc_lo[:])
        nc.vector.tensor_copy(a_rows[0][:, hi], acc_hi[:])
        for s in range(1, PACK):
            acc = first_product(s, s + 1, slice(0, J))
            nc.vector.tensor_copy(a_rows[s][:], acc[:])

        p_rows = [sb_tile("p_rows%d" % i, [P, O], F32) for i in range(N // P)]
        q_rows = [sb_tile("q_rows%d" % i, [P, O], F32) for i in range(N // P)]
        second = []
        for i in range(N // P):
            cols = slice(i * P, (i + 1) * P)
            second.append((wb_w[:, 2 * i * P : 2 * (i + 1) * P].bitcast(FP4X4), wb_s[:, cols], p_rows[i]))
            second.append((wo_w[:, PACK * i * P : PACK * (i + 1) * P].bitcast(FP8X4), wo_s[:, cols], q_rows[i]))

        hid_q = []
        for h in range(2):
            hid_words = sb_tile("hid_words%d" % h, [P, HALF, PACK], BF16)
            part = slice(h * HALF // LIST, (h + 1) * HALF // LIST)
            for s0 in range(0, PACK, 2):
                shared = keep.tile([P, 2, HALF], F32, name="shared%d_%d" % (h, s0), tag="shared%d" % s0)
                own = keep.tile([P, 2, HALF], F32, name="own%d_%d" % (h, s0), tag="own%d" % s0)
                for s in range(s0, s0 + 2):
                    gather(shared[:, s - s0, :], a_rows[s], l4[:, part], sa_t[:, s : s + 1])
                    gather(own[:, s - s0, :], a_rows[s], l5[:, part], sb_t[:, s : s + 1])
                nc.vector.tensor_tensor(
                    hid_words[:, :, s0 : s0 + 2],
                    shared[:].rearrange("p s o -> p o s"),
                    own[:].rearrange("p s o -> p o s"),
                    ALU.max,
                )
            hid_q.append(quantise("hid%d" % h, hid_words, HALF))

        def second_product(acc, m, h):
            nc.tensor.matmul_mx(
                out=acc,
                lhsT=second[m][0], lhsT_scale=second[m][1],
                rhs=hid_q[h][0][:].bitcast(FP8X4), rhs_scale=hid_q[h][1][:],
                start=True, stop=True,
            )

        early = psum.tile([P, len(second), HALF], F32, name="early", tag="bank5")
        for m in range(len(second)):
            second_product(early[:, m, :], m, 0)
        for m in range(len(second)):
            nc.scalar.copy(second[m][2][:, 0:HALF], early[:, m, :])
        for m in range(len(second)):
            late = psum.tile([P, HALF], F32, name="late%d" % m, tag="bank%d" % ((6 + m) % 8))
            second_product(late[:], m, 1)
            nc.vector.tensor_copy(second[m][2][:, HALF:O], late[:])

        for i in range(N // P):
            p_pick = sb_tile("p_pick%d" % i, [P, U], F32)
            q_pick = sb_tile("q_pick%d" % i, [P, U], F32)
            res = sb_tile("res%d" % i, [P, U], F32)
            gather(p_pick[:], p_rows[i], l6[:], so_t[:, i, :])
            gather(q_pick[:], q_rows[i], l7[:], sp_t[:, i, :])
            nc.vector.tensor_tensor(res[:], p_pick[:], q_pick[:], ALU.subtract)
            nc.sync.dma_start(out[i * P : (i + 1) * P, :], res[:])
